import numpy as np
import ml_dtypes


def mxq(x, axis, fmt="e4m3"):
    dtype, down = {"e4m3": (ml_dtypes.float8_e4m3fn, 7), "e5m2": (ml_dtypes.float8_e5m2, 14)}[fmt]
    v = np.moveaxis(np.asarray(x, np.float32).astype(ml_dtypes.bfloat16).astype(np.float64), axis, -1)
    blocks = v.reshape(v.shape[:-1] + (-1, 32))
    amax = np.abs(blocks).max(-1, keepdims=True)
    byte = np.maximum(np.where(amax > 0, np.frexp(amax)[1] - 1 + 127, 0) - down, 1)
    scale = np.exp2(byte - 127.0)
    codes = (blocks / scale).astype(np.float32).astype(dtype).astype(np.float64)
    return np.moveaxis((codes * scale).reshape(v.shape), -1, axis)


WIDE = False


def mx_kscale(k):
    if not WIDE:
        return np.ones(k)
    levels = np.array([10, -10, 5, -5, 0])
    if k % 512:
        return np.exp2(np.random.permutation(np.resize(levels, k // 32))).repeat(32)
    a = np.empty((k // 512, 16))
    for p in range(k // 512):
        a[p, :8] = np.random.permutation(np.resize(levels, 8))
        for g in range(8):
            far = levels[np.abs(levels - a[p, g]) >= 10]
            a[p, g + 8] = far[np.random.randint(len(far))]
    return np.exp2(a.ravel()).repeat(32)


def f64(x):
    return np.asarray(x).astype(np.float64)


def striped(idx):
    return np.tile(idx.reshape(-1, 16).T, (8, 1)).astype(np.uint16)


def unstriped(offs):
    return offs[:16].T.reshape(-1).astype(np.int64)


E2M1 = np.array([0.0, 0.5, 1.0, 1.5, 2.0, 3.0, 4.0, 6.0, -0.0, -0.5, -1.0, -1.5, -2.0, -3.0, -4.0, -6.0])


def pack_weight(w, fmt):
    k, n = w.shape
    w = f64(np.asarray(w, np.float32).astype(ml_dtypes.bfloat16)).reshape(k // 32, 32, n)
    amax = np.abs(w).max(1)
    if fmt == "e4m3":
        byte = np.frexp(amax)[1] - 1 + 127 - 7
    else:
        mant, ex = np.frexp(amax / 6.0)
        byte = np.where(mant > 0.5, ex, ex - 1) + 127
    byte = np.clip(np.where(amax > 0, byte, 1), 1, 254)
    scaled = (w * np.exp2(127.0 - byte)[:, None, :]).reshape(k, n).astype(np.float32)
    by_word = np.ascontiguousarray(scaled.reshape(k // 512, 128, 4, n).transpose(0, 1, 3, 2))
    if fmt == "e4m3":
        words = by_word.astype(ml_dtypes.float8_e4m3fn).view(np.uint8)
    else:
        c = by_word.astype(ml_dtypes.float4_e2m1fn).view(np.uint8) & 0xF
        words = (c[..., 0::2] | (c[..., 1::2] << 4)).reshape(k // 512, 128, 2 * n)
    return np.ascontiguousarray(words), np.ascontiguousarray(byte.astype(np.uint8).reshape(k // 512, 16, n))


def unpack_weight(words, scales, fmt):
    g, _, n = scales.shape
    words = np.ascontiguousarray(words).reshape(g, 128, n, -1)
    if fmt == "e4m3":
        vals = words.view(ml_dtypes.float8_e4m3fn).astype(np.float64)
    else:
        nib = np.empty((g, 128, n, 4), np.uint8)
        nib[..., 0::2] = words & 0xF
        nib[..., 1::2] = words >> 4
        vals = E2M1[nib]
    vals = vals * np.repeat(np.exp2(scales.astype(np.float64) - 127.0), 8, axis=1)[..., None]
    return vals.transpose(0, 1, 3, 2).reshape(g * 512, n)


def gelu(v):
    return 0.5 * v * (1.0 + np.tanh(np.sqrt(2.0 / np.pi) * (v + 0.044715 * v**3)))


def bf(x):
    return np.asarray(x, np.float32).astype(ml_dtypes.bfloat16)


def planes(Y):
    n, m = Y.shape
    b = f64(bf(Y)).reshape(n // 32, 32, m)
    amax = np.abs(b).max(1)
    byte = np.clip(np.where(amax > 0, np.frexp(amax)[1] - 1 + 127 - 7, 1), 1, 254)
    codes = (b * np.exp2(127.0 - byte)[:, None, :]).reshape(n, m).astype(np.float32).astype(ml_dtypes.float8_e4m3fn).view(np.uint8)
    words = codes.reshape(n // 512, 128, 4, m).transpose(0, 1, 3, 2)
    return np.ascontiguousarray(words), np.ascontiguousarray(byte.astype(np.uint8).reshape(n // 512, 16, m))


K, T, S, P, H, N = 1024, 4096, 1024, 512, 1024, 512

def setup_inputs():
    n = np.random.standard_normal
    s = mx_kscale(K)[:, None]
    u = mx_kscale(H)[:, None]
    tab_words, tab_scales = pack_weight(n((K, T)) * s, "e4m3")
    w1 = (n((K, H)) / np.sqrt(K) / s * u.T).astype(np.float32)
    low = ((-0.6 + 0.4 * n(H)) * u[:, 0]).astype(np.float32)
    wa = (1.15 * n((H, N)) / np.sqrt(H) / u).astype(np.float32)
    wb_words, wb_scales = pack_weight(1.9 * n((H, N)) / np.sqrt(H) / u, "e2m1")
    thr = n(N).astype(np.float32)
    sg = (np.sign(n(N)) * np.random.uniform(2.0, 4.0, N)).astype(np.float32)
    gain = (0.5 * np.exp(0.8 * n(N))).astype(np.float32)
    return {"tab_words": tab_words, "tab_scales": tab_scales,
            "offs": striped(np.random.permutation(T)[:S]),
            "pos1": striped(np.random.permutation(S)[:P]),
            "pos2": striped(np.random.permutation(S)[:P]),
            "w1": w1, "low": low, "wa": wa,
            "wb_words": wb_words, "wb_scales": wb_scales,
            "thr": thr, "sg": sg, "gain": gain}

def reference(tab_words, tab_scales, offs, pos1, pos2, w1, low, wa, wb_words, wb_scales, thr, sg, gain):
    v = unpack_weight(tab_words, tab_scales, "e4m3")[:, unstriped(offs)]
    w1q = mxq(f64(w1), 0, "e4m3")
    h = np.maximum(w1q.T @ v, f64(low)[:, None])
    hq = mxq(h, 0, "e4m3")
    waq = mxq(f64(wa), 0, "e4m3")
    wb = unpack_weight(wb_words, wb_scales, "e2m1")
    e = waq.T @ hq
    d = np.tanh(wb.T @ hq) + e
    a = 1.0 / (1.0 + np.exp(-(e[:, unstriped(pos1)] + f64(thr)[:, None])))
    c = d[:, unstriped(pos2)]
    y = f64(gain)[:, None] * (f64(sg)[:, None] * a + c)
    words, scales = planes(y)
    return y, words, scales

@@ -1,0 +1,276 @@
+from contextlib import ExitStack
+
+import concourse.mybir as mybir
+
+K, T, S, M, H, N = 1024, 4096, 1024, 512, 1024, 512
+FLOPS = 2 * K * H * S + 2 * 2 * H * N * S
+
+F32 = mybir.dt.float32
+BF16 = mybir.dt.bfloat16
+I32 = mybir.dt.int32
+U32 = mybir.dt.uint32
+U16 = mybir.dt.uint16
+U8 = mybir.dt.uint8
+FP8X4 = mybir.dt.float8_e4m3fn_x4
+FP4X4 = mybir.dt.float4_e2m1fn_x4
+ALU = mybir.AluOpType
+ACT = mybir.ActivationFunctionType
+
+P = 128
+PACK = 4
+PASS = P * PACK
+BANK = 512
+CHUNK = BANK // PACK
+VECTOR_SHARE = 42
+
+
+def tile_list_depot_balance_features_kernel(
+    tc, tab_words, tab_scales, offs, pos1, pos2, w1, low, wa, wb_words, wb_scales, thr, sg, gain, out_0, out_1, out_2
+):
+    nc = tc.nc
+    with ExitStack() as ctx:
+        keep = ctx.enter_context(tc.tile_pool(name="keep", bufs=1))
+        ring = ctx.enter_context(tc.tile_pool(name="ring", bufs=3))
+        psum = ctx.enter_context(tc.psum_pool(name="psum", bufs=8))
+
+        def held(name, shape, dtype):
+            return keep.tile(shape, dtype, name=name, align_bytes=64)
+
+        offs_sb = held("offs_sb", [P, S // 16], U16)
+        pos1_sb = held("pos1_sb", [P, M // 16], U16)
+        pos2_sb = held("pos2_sb", [P, M // 16], U16)
+        tabw = [keep.tile([P, T], I32, name=f"tabw{a}", tag=f"table{a}", align_bytes=64) for a in range(2)]
+        tabs = held("tabs", [P, T], U8)
+        wbw_raw = held("wbw_raw", [P, 2, 2 * N], U8)
+        wbs_raw = held("wbs_raw", [P, 2, N], U8)
+        low_sb = held("low_sb", [P, 2, PACK], F32)
+        thr_sb = held("thr_sb", [P, PACK], F32)
+        sg_sb = held("sg_sb", [P, PACK], F32)
+        gain_sb = held("gain_sb", [P, PACK], F32)
+
+        nc.vector.memset(tabs[:].bitcast(I32), 0)
+        nc.gpsimd.memset(wbs_raw[:].rearrange("p a c -> p (a c)").bitcast(I32), 0)
+
+        def load_rows(name, rows):
+            raw = held(name, [P, PACK, rows.shape[1]], F32)
+            nc.sync.dma_start(out=raw[:], in_=rows.rearrange("(p j) c -> p j c", j=PACK))
+            return raw
+
+        def load_table(a):
+            nc.sync.dma_start(out=tabw[a][:], in_=tab_words[a].rearrange("p t i -> p (t i)").bitcast(I32))
+
+        nc.sync.dma_start(offs_sb[:], offs)
+        nc.sync.dma_start(out=wbw_raw[:].bitcast(I32), in_=wb_words.rearrange("a p c -> p a c").bitcast(I32))
+        load_table(0)
+        for q in range(4):
+            nc.gpsimd.dma_start(
+                out=wbs_raw[32 * q : 32 * q + 4, :, :].bitcast(I32),
+                in_=wb_scales[:, 4 * q : 4 * q + 4, :].rearrange("a r c -> r a c").bitcast(I32),
+            )
+        for q in range(4):
+            nc.sync.dma_start(
+                out=tabs[32 * q : 32 * q + 8, :].bitcast(I32),
+                in_=tab_scales[:, 4 * q : 4 * q + 4, :].bitcast(I32),
+            )
+        nc.sync.dma_start(out=low_sb[:], in_=low.rearrange("(b p t) -> p b t", b=2, t=PACK))
+        w1_00 = load_rows("w1_00", w1[:PASS, :PASS])
+        load_table(1)
+        w1_10 = [load_rows(f"w1_10{i}", w1[PASS:, i * PASS // 2 : (i + 1) * PASS // 2]) for i in range(2)]
+        w1_01 = load_rows("w1_01", w1[:PASS, PASS:])
+        w1_11 = load_rows("w1_11", w1[PASS:, PASS:])
+        wa_raw = [load_rows(f"wa_raw{b}", wa[b * PASS : (b + 1) * PASS, :]) for b in range(2)]
+        for dst, vec in ((thr_sb, thr), (sg_sb, sg), (gain_sb, gain)):
+            nc.sync.dma_start(out=dst[:], in_=vec.rearrange("(p t) -> p t", t=PACK))
+        nc.sync.dma_start(pos1_sb[:], pos1)
+        nc.sync.dma_start(pos2_sb[:], pos2)
+
+        wbw = held("wbw", [P, 2, 2 * N], U8)
+        nc.vector.tensor_copy(
+            out=wbw[:].rearrange("p a (t m e) -> p a t m e", t=PACK, e=2),
+            in_=wbw_raw[:].rearrange("p a (m t e) -> p a t m e", t=PACK, e=2),
+        )
+
+        def new_dealt():
+            return ring.tile([P, PASS * PACK], BF16, name="dealt", align_bytes=64)
+
+        def round_columns(copy, dealt, raw, first, lo, hi):
+            dst = dealt[:].rearrange("p (t m j) -> p m j t", t=PACK, j=PACK)
+            src = raw[:].rearrange("p j (m t) -> p m j t", t=PACK)
+            copy(out=dst[:, first + lo : first + hi], in_=src[:, lo:hi])
+
+        def round_weight(raw):
+            dealt = new_dealt()
+            round_columns(nc.scalar.copy, dealt, raw, 0, 0, P)
+            return dealt
+
+        def quantise(name, rounded):
+            words = held(name + "_words", [P, BANK], U32)
+            plane = held(name + "_plane", [P, BANK], U8)
+            nc.vector.quantize_mx(out=words[:].bitcast(FP8X4), scales=plane[:], in_=rounded)
+            return words, plane
+
+        vw = [held(f"vw{a}", [P, S], U32) for a in range(2)]
+        vs = held("vs", [P, S], U8)
+        hq = {}
+
+        def first_pass(a, w1q, banks):
+            words, plane = w1q
+            for c, bank in enumerate(banks):
+                cols = slice(c * CHUNK, (c + 1) * CHUNK)
+                for t in range(PACK):
+                    ch = slice(t * P, (t + 1) * P)
+                    nc.tensor.matmul_mx(
+                        out=bank[:, t, :],
+                        lhsT=words[:, ch].bitcast(FP8X4),
+                        lhsT_scale=plane[:, ch],
+                        rhs=vw[a][:, cols].bitcast(FP8X4),
+                        rhs_scale=vs[4 * a : P, cols],
+                        start=(a == 0 and t == 0),
+                        stop=(a == 1 and t == PACK - 1),
+                    )
+
+        def make_h(b, half, banks):
+            hb = ring.tile([P, BANK, PACK], BF16, name="hb", align_bytes=64)
+            for i in range(PACK):
+                nc.vector.tensor_tensor(
+                    out=hb[:, i * CHUNK : (i + 1) * CHUNK, :],
+                    in0=banks[PACK * half + i][:].rearrange("p t n -> p n t"),
+                    in1=low_sb[:, b, :].unsqueeze(1).to_broadcast([P, CHUNK, PACK]),
+                    op=ALU.max,
+                )
+            return hb
+
+        def quantise_h(b, half, hb):
+            hq[b, half] = quantise(f"hq{b}{half}", hb[:].rearrange("p n t -> p (n t)"))
+
+        def new_banks():
+            return [psum.tile([P, PACK, CHUNK], F32, name="acc", tag="acc") for c in range(S // CHUNK)]
+
+        nc.vector.tensor_copy(vw[0][:], tabw[0][:].bitcast(U32).indirect(offs_sb[:]))
+        nc.vector.tensor_copy(vs[:], tabs[:].indirect(offs_sb[:]))
+        banks0 = new_banks()
+        first_pass(0, quantise("w1q00", round_weight(w1_00)[:]), banks0)
+        nc.vector.tensor_copy(vw[1][:], tabw[1][:].bitcast(U32).indirect(offs_sb[:]))
+        dealt10 = new_dealt()
+        round_columns(nc.scalar.copy, dealt10, w1_10[0], 0, 0, P // 2)
+        round_columns(nc.vector.tensor_copy, dealt10, w1_10[1], P // 2, 0, VECTOR_SHARE)
+        round_columns(nc.scalar.copy, dealt10, w1_10[1], P // 2, VECTOR_SHARE, P // 2)
+        first_pass(1, quantise("w1q10", dealt10[:]), banks0)
+        wbs = keep.tile([P, 2, N], U8, name="wbs", tag="table1", align_bytes=64)
+        nc.vector.tensor_copy(
+            out=wbs[:].rearrange("p a (t m) -> p a t m", t=PACK),
+            in_=wbs_raw[:].rearrange("p a (m t) -> p a t m", t=PACK),
+        )
+
+        dealt01 = round_weight(w1_01)
+        hb00 = make_h(0, 0, banks0)
+        dealt11 = round_weight(w1_11)
+        banks1 = new_banks()
+        w1q01 = quantise("w1q01", dealt01[:])
+        hb01 = make_h(0, 1, banks0)
+        first_pass(0, w1q01, banks1)
+        first_pass(1, quantise("w1q11", dealt11[:]), banks1)
+        quantise_h(0, 0, hb00)
+        quantise_h(0, 1, hb01)
+        dealt_a = [round_weight(wa_raw[b]) for b in range(2)]
+        hb10 = make_h(1, 0, banks1)
+        waq = [quantise("waq0", dealt_a[0][:])]
+        quantise_h(1, 0, hb10)
+        waq.append(quantise("waq1", dealt_a[1][:]))
+        hb11 = make_h(1, 1, banks1)
+        quantise_h(1, 1, hb11)
+
+        sgg = held("sgg", [P, PACK], F32)
+        nc.vector.tensor_tensor(out=sgg[:], in0=sg_sb[:], in1=gain_sb[:], op=ALU.mult)
+
+        def second_product(stationary, half):
+            bank = psum.tile([P, BANK], F32, name="acc", tag="acc")
+            for b in range(2):
+                words, plane = hq[b, half]
+                lhs, lhs_plane = stationary(b)
+                nc.tensor.matmul_mx(
+                    out=bank[:],
+                    lhsT=lhs,
+                    lhsT_scale=lhs_plane,
+                    rhs=words[:].bitcast(FP8X4),
+                    rhs_scale=plane[:],
+                    start=(b == 0),
+                    stop=(b == 1),
+                )
+            return bank
+
+        def correction(t, half):
+            bank = second_product(
+                lambda b: (wbw[:, b, 2 * t * P : 2 * (t + 1) * P].bitcast(FP4X4), wbs[:, b, t * P : (t + 1) * P]), half
+            )
+            th = held(f"th{t}{half}", [P, BANK], F32)
+            nc.scalar.activation(out=th[:], in_=bank[:], func=ACT.Tanh)
+            return th
+
+        def score(t, half):
+            bank = second_product(
+                lambda b: (waq[b][0][:, t * P : (t + 1) * P].bitcast(FP8X4), waq[b][1][:, t * P : (t + 1) * P]), half
+            )
+            nc.scalar.copy(out=e[t][:, half * BANK : (half + 1) * BANK], in_=bank[:])
+
+        def add_correction(t, half, th):
+            cols = slice(half * BANK, (half + 1) * BANK)
+            nc.vector.tensor_tensor(out=d[t][:, cols], in0=th[:], in1=e[t][:, cols], op=ALU.add)
+
+        e = [held(f"e{t}", [P, S], F32) for t in range(PACK)]
+        d = [held(f"d{t}", [P, S], F32) for t in range(PACK)]
+        y = held("y", [P, PACK, M], F32)
+        y_out = out_0.rearrange("(p t) m -> p t m", t=PACK)
+        yb = held("yb", [P, M, PACK], BF16)
+        y_words = held("y_words", [P, M], U32)
+        y_plane = held("y_plane", [P, M], U8)
+        words_out = out_1[0].rearrange("p m t -> p (m t)").bitcast(I32)
+
+        th0 = [correction(t, 0) for t in range(PACK)]
+        for t in range(PACK):
+            score(t, 0)
+        for t in range(PACK):
+            th1 = correction(t, 1)
+            score(t, 1)
+            add_correction(t, 0, th0[t])
+            add_correction(t, 1, th1)
+            pieces = 2 if t == PACK - 1 else 1
+            width = M // pieces
+            for i in range(pieces):
+                cols = slice(i * width, (i + 1) * width)
+                entries = slice(i * width // 16, (i + 1) * width // 16)
+                seen = ring.tile([P, width], F32, name="seen")
+                nc.scalar.activation(
+                    out=seen[:], in_=e[t][:].indirect(pos1_sb[:, entries]), func=ACT.Sigmoid, bias=thr_sb[:, t : t + 1]
+                )
+                weighted = ring.tile([P, width], F32, name="weighted")
+                nc.scalar.activation(out=weighted[:], in_=seen[:], func=ACT.Copy, scale=sgg[:, t : t + 1])
+                picked = ring.tile([P, width], F32, name="picked")
+                nc.vector.tensor_copy(picked[:], d[t][:].indirect(pos2_sb[:, entries]))
+                nc.vector.scalar_tensor_tensor(
+                    out=y[:, t, cols],
+                    in0=picked[:],
+                    scalar=gain_sb[:, t : t + 1],
+                    in1=weighted[:],
+                    op0=ALU.mult,
+                    op1=ALU.add,
+                )
+                nc.sync.dma_start(out=y_out[:, t, cols], in_=y[:, t, cols])
+        for i in range(2):
+            cols = slice(i * M // 2, (i + 1) * M // 2)
+            copy = nc.vector.tensor_copy if i else nc.scalar.copy
+            copy(
+                out=yb[:, cols, :].rearrange("p (c i) t -> p c t i", i=4),
+                in_=y[:, :, cols].rearrange("p t (c i) -> p c t i", i=4),
+            )
+            nc.vector.quantize_mx(
+                out=y_words[:, cols].bitcast(FP8X4),
+                scales=y_plane[:, cols],
+                in_=yb[:, cols, :].rearrange("p m t -> p (m t)"),
+            )
+            nc.sync.dma_start(out=words_out[:, cols], in_=y_words[:, cols].bitcast(I32))
+        for q in range(4):
+            queue = nc.scalar if q % 2 else nc.sync
+            queue.dma_start(
+                out=out_2[0, 4 * q : 4 * q + 4, :].bitcast(I32), in_=y_plane[32 * q : 32 * q + 4, :].bitcast(I32)
+            )

@@ -22,6 +22,7 @@ PASS = P * PACK
 BANK = 512
 CHUNK = BANK // PACK
 VECTOR_SHARE = 42
+VECTOR_WEIGHS = 1
 
 
 def tile_list_depot_balance_features_kernel(
@@ -48,6 +49,9 @@ def tile_list_depot_balance_features_kernel(
         sg_sb = held("sg_sb", [P, PACK], F32)
         gain_sb = held("gain_sb", [P, PACK], F32)
 
+        warm = held("warm", [P, 2], F32)
+        nc.vector.memset(warm[:, 0:1], 0.0)
+        nc.scalar.activation(out=warm[:, 1:2], in_=warm[:, 0:1], func=ACT.Sigmoid)
         nc.vector.memset(tabs[:].bitcast(I32), 0)
         nc.gpsimd.memset(wbs_raw[:].rearrange("p a c -> p (a c)").bitcast(I32), 0)
 
@@ -60,22 +64,22 @@ def tile_list_depot_balance_features_kernel(
             nc.sync.dma_start(out=tabw[a][:], in_=tab_words[a].rearrange("p t i -> p (t i)").bitcast(I32))
 
         nc.sync.dma_start(offs_sb[:], offs)
-        nc.sync.dma_start(out=wbw_raw[:].bitcast(I32), in_=wb_words.rearrange("a p c -> p a c").bitcast(I32))
         load_table(0)
-        for q in range(4):
-            nc.gpsimd.dma_start(
-                out=wbs_raw[32 * q : 32 * q + 4, :, :].bitcast(I32),
-                in_=wb_scales[:, 4 * q : 4 * q + 4, :].rearrange("a r c -> r a c").bitcast(I32),
-            )
         for q in range(4):
             nc.sync.dma_start(
                 out=tabs[32 * q : 32 * q + 8, :].bitcast(I32),
                 in_=tab_scales[:, 4 * q : 4 * q + 4, :].bitcast(I32),
             )
-        nc.sync.dma_start(out=low_sb[:], in_=low.rearrange("(b p t) -> p b t", b=2, t=PACK))
+        for q in range(4):
+            nc.gpsimd.dma_start(
+                out=wbs_raw[32 * q : 32 * q + 4, :, :].bitcast(I32),
+                in_=wb_scales[:, 4 * q : 4 * q + 4, :].rearrange("a r c -> r a c").bitcast(I32),
+            )
         w1_00 = load_rows("w1_00", w1[:PASS, :PASS])
         load_table(1)
         w1_10 = [load_rows(f"w1_10{i}", w1[PASS:, i * PASS // 2 : (i + 1) * PASS // 2]) for i in range(2)]
+        nc.sync.dma_start(out=low_sb[:], in_=low.rearrange("(b p t) -> p b t", b=2, t=PACK))
+        nc.sync.dma_start(out=wbw_raw[:].bitcast(I32), in_=wb_words.rearrange("a p c -> p a c").bitcast(I32))
         w1_01 = load_rows("w1_01", w1[:PASS, PASS:])
         w1_11 = load_rows("w1_11", w1[PASS:, PASS:])
         wa_raw = [load_rows(f"wa_raw{b}", wa[b * PASS : (b + 1) * PASS, :]) for b in range(2)]
@@ -84,14 +88,8 @@ def tile_list_depot_balance_features_kernel(
         nc.sync.dma_start(pos1_sb[:], pos1)
         nc.sync.dma_start(pos2_sb[:], pos2)
 
-        wbw = held("wbw", [P, 2, 2 * N], U8)
-        nc.vector.tensor_copy(
-            out=wbw[:].rearrange("p a (t m e) -> p a t m e", t=PACK, e=2),
-            in_=wbw_raw[:].rearrange("p a (m t e) -> p a t m e", t=PACK, e=2),
-        )
-
         def new_dealt():
-            return ring.tile([P, PASS * PACK], BF16, name="dealt", align_bytes=64)
+            return ring.tile([P, PASS * PACK], BF16, name="dealt", align_bytes=64, bufs=2)
 
         def round_columns(copy, dealt, raw, first, lo, hi):
             dst = dealt[:].rearrange("p (t m j) -> p m j t", t=PACK, j=PACK)
@@ -113,9 +111,9 @@ def tile_list_depot_balance_features_kernel(
         vs = held("vs", [P, S], U8)
         hq = {}
 
-        def first_pass(a, w1q, banks):
+        def first_pass(a, w1q, banks, first=0):
             words, plane = w1q
-            for c, bank in enumerate(banks):
+            for c, bank in enumerate(banks, first):
                 cols = slice(c * CHUNK, (c + 1) * CHUNK)
                 for t in range(PACK):
                     ch = slice(t * P, (t + 1) * P)
@@ -129,26 +127,27 @@ def tile_list_depot_balance_features_kernel(
                         stop=(a == 1 and t == PACK - 1),
                     )
 
-        def make_h(b, half, banks):
-            hb = ring.tile([P, BANK, PACK], BF16, name="hb", align_bytes=64)
-            for i in range(PACK):
+        def new_hb():
+            return ring.tile([P, BANK, PACK], BF16, name="hb", align_bytes=64, bufs=2)
+
+        def make_h(b, banks, hb):
+            for i in range(len(banks)):
                 nc.vector.tensor_tensor(
-                    out=hb[:, i * CHUNK : (i + 1) * CHUNK, :],
-                    in0=banks[PACK * half + i][:].rearrange("p t n -> p n t"),
-                    in1=low_sb[:, b, :].unsqueeze(1).to_broadcast([P, CHUNK, PACK]),
+                    out=hb[:, i * CHUNK : (i + 1) * CHUNK, :].rearrange("p (c u) t -> p c t u", u=2),
+                    in0=banks[i][:].rearrange("p t (c u) -> p c t u", u=2),
+                    in1=low_sb[:, b, :].unsqueeze(1).unsqueeze(3).to_broadcast([P, CHUNK // 2, PACK, 2]),
                     op=ALU.max,
                 )
-            return hb
 
         def quantise_h(b, half, hb):
             hq[b, half] = quantise(f"hq{b}{half}", hb[:].rearrange("p n t -> p (n t)"))
 
-        def new_banks():
-            return [psum.tile([P, PACK, CHUNK], F32, name="acc", tag="acc") for c in range(S // CHUNK)]
+        def new_banks(count):
+            return [psum.tile([P, PACK, CHUNK], F32, name="acc", tag="acc") for c in range(count)]
 
         nc.vector.tensor_copy(vw[0][:], tabw[0][:].bitcast(U32).indirect(offs_sb[:]))
         nc.vector.tensor_copy(vs[:], tabs[:].indirect(offs_sb[:]))
-        banks0 = new_banks()
+        banks0 = new_banks(2 * PACK)
         first_pass(0, quantise("w1q00", round_weight(w1_00)[:]), banks0)
         nc.vector.tensor_copy(vw[1][:], tabw[1][:].bitcast(U32).indirect(offs_sb[:]))
         dealt10 = new_dealt()
@@ -161,27 +160,19 @@ def tile_list_depot_balance_features_kernel(
             out=wbs[:].rearrange("p a (t m) -> p a t m", t=PACK),
             in_=wbs_raw[:].rearrange("p a (m t) -> p a t m", t=PACK),
         )
-
-        dealt01 = round_weight(w1_01)
-        hb00 = make_h(0, 0, banks0)
-        dealt11 = round_weight(w1_11)
-        banks1 = new_banks()
-        w1q01 = quantise("w1q01", dealt01[:])
-        hb01 = make_h(0, 1, banks0)
-        first_pass(0, w1q01, banks1)
-        first_pass(1, quantise("w1q11", dealt11[:]), banks1)
-        quantise_h(0, 0, hb00)
-        quantise_h(0, 1, hb01)
-        dealt_a = [round_weight(wa_raw[b]) for b in range(2)]
-        hb10 = make_h(1, 0, banks1)
-        waq = [quantise("waq0", dealt_a[0][:])]
-        quantise_h(1, 0, hb10)
-        waq.append(quantise("waq1", dealt_a[1][:]))
-        hb11 = make_h(1, 1, banks1)
-        quantise_h(1, 1, hb11)
-
+        wbw = held("wbw", [P, 2, 2 * N], U8)
+        nc.scalar.copy(
+            out=wbw[:].bitcast(U16).rearrange("p a (t m) -> p a t m", t=PACK),
+            in_=wbw_raw[:].bitcast(U16).rearrange("p a (m t) -> p a t m", t=PACK),
+        )
+        dealt_b1 = []
+        for a, raw in enumerate((w1_01, w1_11)):
+            dealt_b1.append(keep.tile([P, PASS * PACK], BF16, name=f"dealt{a}1", tag=f"late{a}", align_bytes=64))
+            round_columns(nc.scalar.copy, dealt_b1[a], raw, 0, 0, P)
+        dealt_a = held("dealt_a", [P, 2 * PASS * PACK], BF16)
+        for b in range(2):
+            round_columns(nc.scalar.copy, dealt_a[:, b * PASS * PACK : (b + 1) * PASS * PACK], wa_raw[b], 0, 0, P)
         sgg = held("sgg", [P, PACK], F32)
-        nc.vector.tensor_tensor(out=sgg[:], in0=sg_sb[:], in1=gain_sb[:], op=ALU.mult)
 
         def second_product(stationary, half):
             bank = psum.tile([P, BANK], F32, name="acc", tag="acc")
@@ -209,7 +200,11 @@ def tile_list_depot_balance_features_kernel(
 
         def score(t, half):
             bank = second_product(
-                lambda b: (waq[b][0][:, t * P : (t + 1) * P].bitcast(FP8X4), waq[b][1][:, t * P : (t + 1) * P]), half
+                lambda b: (
+                    wa_words[:, b * N + t * P : b * N + (t + 1) * P].bitcast(FP8X4),
+                    wa_plane[:, b * N + t * P : b * N + (t + 1) * P],
+                ),
+                half,
             )
             nc.scalar.copy(out=e[t][:, half * BANK : (half + 1) * BANK], in_=bank[:])
 
@@ -226,36 +221,101 @@ def tile_list_depot_balance_features_kernel(
         y_plane = held("y_plane", [P, M], U8)
         words_out = out_1[0].rearrange("p m t -> p (m t)").bitcast(I32)
 
-        th0 = [correction(t, 0) for t in range(PACK)]
+        hb00 = new_hb()
+        make_h(0, banks0[:PACK], hb00)
+        w1q01 = quantise("w1q01", dealt_b1[0][:])
+        banks10 = new_banks(PACK)
+        first_pass(0, w1q01, banks10)
+        hb01 = [keep.tile([P, BANK // 2, PACK], BF16, name=f"hb01{i}", tag=f"late{i}", align_bytes=64) for i in range(2)]
+        make_h(0, banks0[PACK : PACK + 2], hb01[0])
+        w1q11 = quantise("w1q11", dealt_b1[1][:])
+        first_pass(1, w1q11, banks10)
+        banks11 = []
+
+        def both_passes(c):
+            banks11.extend(new_banks(1))
+            first_pass(0, w1q01, banks11[c:], PACK + c)
+            first_pass(1, w1q11, banks11[c:], PACK + c)
+
+        both_passes(0)
+        both_passes(1)
+        quantise_h(0, 0, hb00)
+        hb10 = keep.tile([P, BANK, PACK], BF16, name="hb10", tag="before_wa", align_bytes=64)
+        make_h(1, banks10, hb10)
+        make_h(0, banks0[PACK + 2 : PACK + 3], hb01[1][:, :CHUNK, :])
+        both_passes(2)
+        quantise_h(1, 0, hb10)
+        th0 = [correction(t, 0) for t in range(2)]
+        make_h(0, banks0[PACK + 3 :], hb01[1][:, CHUNK:, :])
+        both_passes(3)
+        th0.extend(correction(t, 0) for t in range(2, PACK))
+        wa_words = keep.tile([P, 2 * N], U32, name="wa_words", tag="before_wa", align_bytes=64)
+        wa_plane = held("wa_plane", [P, 2 * N], U8)
+        nc.vector.quantize_mx(out=wa_words[:].bitcast(FP8X4), scales=wa_plane[:], in_=dealt_a[:])
         for t in range(PACK):
             score(t, 0)
-        for t in range(PACK):
+        hq[0, 1] = held("hq01_words", [P, BANK], U32), held("hq01_plane", [P, BANK], U8)
+        for i in range(2):
+            cols = slice(i * BANK // 2, (i + 1) * BANK // 2)
+            nc.vector.quantize_mx(
+                out=hq[0, 1][0][:, cols].bitcast(FP8X4),
+                scales=hq[0, 1][1][:, cols],
+                in_=hb01[i][:].rearrange("p n t -> p (n t)"),
+            )
+        hb11 = new_hb()
+        make_h(1, banks11, hb11)
+        nc.vector.tensor_tensor(out=sgg[:], in0=sg_sb[:], in1=gain_sb[:], op=ALU.mult)
+        add_correction(0, 0, th0[0])
+        quantise_h(1, 1, hb11)
+        for t in range(1, PACK):
+            add_correction(t, 0, th0[t])
+
+        def finish_rows(t):
             th1 = correction(t, 1)
             score(t, 1)
-            add_correction(t, 0, th0[t])
             add_correction(t, 1, th1)
-            pieces = 2 if t == PACK - 1 else 1
-            width = M // pieces
-            for i in range(pieces):
-                cols = slice(i * width, (i + 1) * width)
-                entries = slice(i * width // 16, (i + 1) * width // 16)
-                seen = ring.tile([P, width], F32, name="seen")
-                nc.scalar.activation(
-                    out=seen[:], in_=e[t][:].indirect(pos1_sb[:, entries]), func=ACT.Sigmoid, bias=thr_sb[:, t : t + 1]
+
+        def look(t, cols):
+            entries = slice(cols.start // 16, cols.stop // 16)
+            seen = ring.tile([P, cols.stop - cols.start], F32, name="seen")
+            nc.scalar.activation(
+                out=seen[:], in_=e[t][:].indirect(pos1_sb[:, entries]), func=ACT.Sigmoid, bias=thr_sb[:, t : t + 1]
+            )
+            weighted = ring.tile([P, cols.stop - cols.start], F32, name="weighted")
+            if t < VECTOR_WEIGHS:
+                nc.vector.tensor_scalar(
+                    out=weighted[:], in0=seen[:], scalar1=sgg[:, t : t + 1], scalar2=None, op0=ALU.mult
                 )
-                weighted = ring.tile([P, width], F32, name="weighted")
+            else:
                 nc.scalar.activation(out=weighted[:], in_=seen[:], func=ACT.Copy, scale=sgg[:, t : t + 1])
-                picked = ring.tile([P, width], F32, name="picked")
-                nc.vector.tensor_copy(picked[:], d[t][:].indirect(pos2_sb[:, entries]))
-                nc.vector.scalar_tensor_tensor(
-                    out=y[:, t, cols],
-                    in0=picked[:],
-                    scalar=gain_sb[:, t : t + 1],
-                    in1=weighted[:],
-                    op0=ALU.mult,
-                    op1=ALU.add,
-                )
-                nc.sync.dma_start(out=y_out[:, t, cols], in_=y[:, t, cols])
+            return weighted
+
+        def pick(t, cols):
+            picked = ring.tile([P, cols.stop - cols.start], F32, name="picked")
+            nc.vector.tensor_copy(picked[:], d[t][:].indirect(pos2_sb[:, cols.start // 16 : cols.stop // 16]))
+            return picked
+
+        def combine(t, cols, picked, weighted):
+            nc.vector.scalar_tensor_tensor(
+                out=y[:, t, cols],
+                in0=picked[:],
+                scalar=gain_sb[:, t : t + 1],
+                in1=weighted[:],
+                op0=ALU.mult,
+                op1=ALU.add,
+            )
+            nc.sync.dma_start(out=y_out[:, t, cols], in_=y[:, t, cols])
+
+        whole = slice(0, M)
+        halves = [slice(0, M // 2), slice(M // 2, M)]
+        finish_rows(0)
+        for t in range(PACK - 1):
+            picked = pick(t, whole)
+            finish_rows(t + 1)
+            combine(t, whole, picked, look(t, whole))
+        picked = [pick(PACK - 1, cols) for cols in halves]
+        for i, cols in enumerate(halves):
+            combine(PACK - 1, cols, picked[i], look(PACK - 1, cols))
         for i in range(2):
             cols = slice(i * M // 2, (i + 1) * M // 2)
             copy = nc.vector.tensor_copy if i else nc.scalar.copy

@@ -53,7 +53,7 @@ def tile_list_depot_balance_features_kernel(
         nc.vector.memset(warm[:, 0:1], 0.0)
         nc.scalar.activation(out=warm[:, 1:2], in_=warm[:, 0:1], func=ACT.Sigmoid)
         nc.vector.memset(tabs[:].bitcast(I32), 0)
-        nc.gpsimd.memset(wbs_raw[:].rearrange("p a c -> p (a c)").bitcast(I32), 0)
+        nc.vector.memset(wbs_raw[:].rearrange("p a c -> p (a c)").bitcast(I32), 0)
 
         def load_rows(name, rows):
             raw = held(name, [P, PACK, rows.shape[1]], F32)
@@ -66,7 +66,7 @@ def tile_list_depot_balance_features_kernel(
         nc.sync.dma_start(offs_sb[:], offs)
         load_table(0)
         for q in range(4):
-            nc.sync.dma_start(
+            nc.gpsimd.dma_start(
                 out=tabs[32 * q : 32 * q + 8, :].bitcast(I32),
                 in_=tab_scales[:, 4 * q : 4 * q + 4, :].bitcast(I32),
             )

from contextlib import ExitStack

import concourse.mybir as mybir

K, T, S, M, H, N = 1024, 4096, 1024, 512, 1024, 512
FLOPS = 2 * K * H * S + 2 * 2 * H * N * S

F32 = mybir.dt.float32
BF16 = mybir.dt.bfloat16
I32 = mybir.dt.int32
U32 = mybir.dt.uint32
U16 = mybir.dt.uint16
U8 = mybir.dt.uint8
FP8X4 = mybir.dt.float8_e4m3fn_x4
FP4X4 = mybir.dt.float4_e2m1fn_x4
ALU = mybir.AluOpType
ACT = mybir.ActivationFunctionType

P = 128
PACK = 4
PASS = P * PACK
BANK = 512
CHUNK = BANK // PACK
VECTOR_SHARE = 42
VECTOR_WEIGHS = 1


def tile_list_depot_balance_features_kernel(
    tc, tab_words, tab_scales, offs, pos1, pos2, w1, low, wa, wb_words, wb_scales, thr, sg, gain, out_0, out_1, out_2
):
    nc = tc.nc
    with ExitStack() as ctx:
        keep = ctx.enter_context(tc.tile_pool(name="keep", bufs=1))
        ring = ctx.enter_context(tc.tile_pool(name="ring", bufs=3))
        psum = ctx.enter_context(tc.psum_pool(name="psum", bufs=8))

        def held(name, shape, dtype):
            return keep.tile(shape, dtype, name=name, align_bytes=64)

        offs_sb = held("offs_sb", [P, S // 16], U16)
        pos1_sb = held("pos1_sb", [P, M // 16], U16)
        pos2_sb = held("pos2_sb", [P, M // 16], U16)
        tabw = [keep.tile([P, T], I32, name=f"tabw{a}", tag=f"table{a}", align_bytes=64) for a in range(2)]
        tabs = held("tabs", [P, T], U8)
        wbw_raw = held("wbw_raw", [P, 2, 2 * N], U8)
        wbs_raw = held("wbs_raw", [P, 2, N], U8)
        low_sb = held("low_sb", [P, 2, PACK], F32)
        thr_sb = held("thr_sb", [P, PACK], F32)
        sg_sb = held("sg_sb", [P, PACK], F32)
        gain_sb = held("gain_sb", [P, PACK], F32)

        warm = held("warm", [P, 2], F32)
        nc.vector.memset(warm[:, 0:1], 0.0)
        nc.scalar.activation(out=warm[:, 1:2], in_=warm[:, 0:1], func=ACT.Sigmoid)
        nc.vector.memset(tabs[:].bitcast(I32), 0)
        nc.vector.memset(wbs_raw[:].rearrange("p a c -> p (a c)").bitcast(I32), 0)

        def load_rows(name, rows):
            raw = held(name, [P, PACK, rows.shape[1]], F32)
            nc.sync.dma_start(out=raw[:], in_=rows.rearrange("(p j) c -> p j c", j=PACK))
            return raw

        def load_table(a):
            nc.sync.dma_start(out=tabw[a][:], in_=tab_words[a].rearrange("p t i -> p (t i)").bitcast(I32))

        nc.sync.dma_start(offs_sb[:], offs)
        load_table(0)
        for q in range(4):
            nc.gpsimd.dma_start(
                out=tabs[32 * q : 32 * q + 8, :].bitcast(I32),
                in_=tab_scales[:, 4 * q : 4 * q + 4, :].bitcast(I32),
            )
        for q in range(4):
            nc.gpsimd.dma_start(
                out=wbs_raw[32 * q : 32 * q + 4, :, :].bitcast(I32),
                in_=wb_scales[:, 4 * q : 4 * q + 4, :].rearrange("a r c -> r a c").bitcast(I32),
            )
        w1_00 = load_rows("w1_00", w1[:PASS, :PASS])
        load_table(1)
        w1_10 = [load_rows(f"w1_10{i}", w1[PASS:, i * PASS // 2 : (i + 1) * PASS // 2]) for i in range(2)]
        nc.sync.dma_start(out=low_sb[:], in_=low.rearrange("(b p t) -> p b t", b=2, t=PACK))
        nc.sync.dma_start(out=wbw_raw[:].bitcast(I32), in_=wb_words.rearrange("a p c -> p a c").bitcast(I32))
        w1_01 = load_rows("w1_01", w1[:PASS, PASS:])
        w1_11 = load_rows("w1_11", w1[PASS:, PASS:])
        wa_raw = [load_rows(f"wa_raw{b}", wa[b * PASS : (b + 1) * PASS, :]) for b in range(2)]
        for dst, vec in ((thr_sb, thr), (sg_sb, sg), (gain_sb, gain)):
            nc.sync.dma_start(out=dst[:], in_=vec.rearrange("(p t) -> p t", t=PACK))
        nc.sync.dma_start(pos1_sb[:], pos1)
        nc.sync.dma_start(pos2_sb[:], pos2)

        def new_dealt():
            return ring.tile([P, PASS * PACK], BF16, name="dealt", align_bytes=64, bufs=2)

        def round_columns(copy, dealt, raw, first, lo, hi):
            dst = dealt[:].rearrange("p (t m j) -> p m j t", t=PACK, j=PACK)
            src = raw[:].rearrange("p j (m t) -> p m j t", t=PACK)
            copy(out=dst[:, first + lo : first + hi], in_=src[:, lo:hi])

        def round_weight(raw):
            dealt = new_dealt()
            round_columns(nc.scalar.copy, dealt, raw, 0, 0, P)
            return dealt

        def quantise(name, rounded):
            words = held(name + "_words", [P, BANK], U32)
            plane = held(name + "_plane", [P, BANK], U8)
            nc.vector.quantize_mx(out=words[:].bitcast(FP8X4), scales=plane[:], in_=rounded)
            return words, plane

        vw = [held(f"vw{a}", [P, S], U32) for a in range(2)]
        vs = held("vs", [P, S], U8)
        hq = {}

        def first_pass(a, w1q, banks, first=0):
            words, plane = w1q
            for c, bank in enumerate(banks, first):
                cols = slice(c * CHUNK, (c + 1) * CHUNK)
                for t in range(PACK):
                    ch = slice(t * P, (t + 1) * P)
                    nc.tensor.matmul_mx(
                        out=bank[:, t, :],
                        lhsT=words[:, ch].bitcast(FP8X4),
                        lhsT_scale=plane[:, ch],
                        rhs=vw[a][:, cols].bitcast(FP8X4),
                        rhs_scale=vs[4 * a : P, cols],
                        start=(a == 0 and t == 0),
                        stop=(a == 1 and t == PACK - 1),
                    )

        def new_hb():
            return ring.tile([P, BANK, PACK], BF16, name="hb", align_bytes=64, bufs=2)

        def make_h(b, banks, hb):
            for i in range(len(banks)):
                nc.vector.tensor_tensor(
                    out=hb[:, i * CHUNK : (i + 1) * CHUNK, :].rearrange("p (c u) t -> p c t u", u=2),
                    in0=banks[i][:].rearrange("p t (c u) -> p c t u", u=2),
                    in1=low_sb[:, b, :].unsqueeze(1).unsqueeze(3).to_broadcast([P, CHUNK // 2, PACK, 2]),
                    op=ALU.max,
                )

        def quantise_h(b, half, hb):
            hq[b, half] = quantise(f"hq{b}{half}", hb[:].rearrange("p n t -> p (n t)"))

        def new_banks(count):
            return [psum.tile([P, PACK, CHUNK], F32, name="acc", tag="acc") for c in range(count)]

        nc.vector.tensor_copy(vw[0][:], tabw[0][:].bitcast(U32).indirect(offs_sb[:]))
        nc.vector.tensor_copy(vs[:], tabs[:].indirect(offs_sb[:]))
        banks0 = new_banks(2 * PACK)
        first_pass(0, quantise("w1q00", round_weight(w1_00)[:]), banks0)
        nc.vector.tensor_copy(vw[1][:], tabw[1][:].bitcast(U32).indirect(offs_sb[:]))
        dealt10 = new_dealt()
        round_columns(nc.scalar.copy, dealt10, w1_10[0], 0, 0, P // 2)
        round_columns(nc.vector.tensor_copy, dealt10, w1_10[1], P // 2, 0, VECTOR_SHARE)
        round_columns(nc.scalar.copy, dealt10, w1_10[1], P // 2, VECTOR_SHARE, P // 2)
        first_pass(1, quantise("w1q10", dealt10[:]), banks0)
        wbs = keep.tile([P, 2, N], U8, name="wbs", tag="table1", align_bytes=64)
        nc.vector.tensor_copy(
            out=wbs[:].rearrange("p a (t m) -> p a t m", t=PACK),
            in_=wbs_raw[:].rearrange("p a (m t) -> p a t m", t=PACK),
        )
        wbw = held("wbw", [P, 2, 2 * N], U8)
        nc.scalar.copy(
            out=wbw[:].bitcast(U16).rearrange("p a (t m) -> p a t m", t=PACK),
            in_=wbw_raw[:].bitcast(U16).rearrange("p a (m t) -> p a t m", t=PACK),
        )
        dealt_b1 = []
        for a, raw in enumerate((w1_01, w1_11)):
            dealt_b1.append(keep.tile([P, PASS * PACK], BF16, name=f"dealt{a}1", tag=f"late{a}", align_bytes=64))
            round_columns(nc.scalar.copy, dealt_b1[a], raw, 0, 0, P)
        dealt_a = held("dealt_a", [P, 2 * PASS * PACK], BF16)
        for b in range(2):
            round_columns(nc.scalar.copy, dealt_a[:, b * PASS * PACK : (b + 1) * PASS * PACK], wa_raw[b], 0, 0, P)
        sgg = held("sgg", [P, PACK], F32)

        def second_product(stationary, half):
            bank = psum.tile([P, BANK], F32, name="acc", tag="acc")
            for b in range(2):
                words, plane = hq[b, half]
                lhs, lhs_plane = stationary(b)
                nc.tensor.matmul_mx(
                    out=bank[:],
                    lhsT=lhs,
                    lhsT_scale=lhs_plane,
                    rhs=words[:].bitcast(FP8X4),
                    rhs_scale=plane[:],
                    start=(b == 0),
                    stop=(b == 1),
                )
            return bank

        def correction(t, half):
            bank = second_product(
                lambda b: (wbw[:, b, 2 * t * P : 2 * (t + 1) * P].bitcast(FP4X4), wbs[:, b, t * P : (t + 1) * P]), half
            )
            th = held(f"th{t}{half}", [P, BANK], F32)
            nc.scalar.activation(out=th[:], in_=bank[:], func=ACT.Tanh)
            return th

        def score(t, half):
            bank = second_product(
                lambda b: (
                    wa_words[:, b * N + t * P : b * N + (t + 1) * P].bitcast(FP8X4),
                    wa_plane[:, b * N + t * P : b * N + (t + 1) * P],
                ),
                half,
            )
            nc.scalar.copy(out=e[t][:, half * BANK : (half + 1) * BANK], in_=bank[:])

        def add_correction(t, half, th):
            cols = slice(half * BANK, (half + 1) * BANK)
            nc.vector.tensor_tensor(out=d[t][:, cols], in0=th[:], in1=e[t][:, cols], op=ALU.add)

        e = [held(f"e{t}", [P, S], F32) for t in range(PACK)]
        d = [held(f"d{t}", [P, S], F32) for t in range(PACK)]
        y = held("y", [P, PACK, M], F32)
        y_out = out_0.rearrange("(p t) m -> p t m", t=PACK)
        yb = held("yb", [P, M, PACK], BF16)
        y_words = held("y_words", [P, M], U32)
        y_plane = held("y_plane", [P, M], U8)
        words_out = out_1[0].rearrange("p m t -> p (m t)").bitcast(I32)

        hb00 = new_hb()
        make_h(0, banks0[:PACK], hb00)
        w1q01 = quantise("w1q01", dealt_b1[0][:])
        banks10 = new_banks(PACK)
        first_pass(0, w1q01, banks10)
        hb01 = [keep.tile([P, BANK // 2, PACK], BF16, name=f"hb01{i}", tag=f"late{i}", align_bytes=64) for i in range(2)]
        make_h(0, banks0[PACK : PACK + 2], hb01[0])
        w1q11 = quantise("w1q11", dealt_b1[1][:])
        first_pass(1, w1q11, banks10)
        banks11 = []

        def both_passes(c):
            banks11.extend(new_banks(1))
            first_pass(0, w1q01, banks11[c:], PACK + c)
            first_pass(1, w1q11, banks11[c:], PACK + c)

        both_passes(0)
        both_passes(1)
        quantise_h(0, 0, hb00)
        hb10 = keep.tile([P, BANK, PACK], BF16, name="hb10", tag="before_wa", align_bytes=64)
        make_h(1, banks10, hb10)
        make_h(0, banks0[PACK + 2 : PACK + 3], hb01[1][:, :CHUNK, :])
        both_passes(2)
        quantise_h(1, 0, hb10)
        th0 = [correction(t, 0) for t in range(2)]
        make_h(0, banks0[PACK + 3 :], hb01[1][:, CHUNK:, :])
        both_passes(3)
        th0.extend(correction(t, 0) for t in range(2, PACK))
        wa_words = keep.tile([P, 2 * N], U32, name="wa_words", tag="before_wa", align_bytes=64)
        wa_plane = held("wa_plane", [P, 2 * N], U8)
        nc.vector.quantize_mx(out=wa_words[:].bitcast(FP8X4), scales=wa_plane[:], in_=dealt_a[:])
        for t in range(PACK):
            score(t, 0)
        hq[0, 1] = held("hq01_words", [P, BANK], U32), held("hq01_plane", [P, BANK], U8)
        for i in range(2):
            cols = slice(i * BANK // 2, (i + 1) * BANK // 2)
            nc.vector.quantize_mx(
                out=hq[0, 1][0][:, cols].bitcast(FP8X4),
                scales=hq[0, 1][1][:, cols],
                in_=hb01[i][:].rearrange("p n t -> p (n t)"),
            )
        hb11 = new_hb()
        make_h(1, banks11, hb11)
        nc.vector.tensor_tensor(out=sgg[:], in0=sg_sb[:], in1=gain_sb[:], op=ALU.mult)
        add_correction(0, 0, th0[0])
        quantise_h(1, 1, hb11)
        for t in range(1, PACK):
            add_correction(t, 0, th0[t])

        def finish_rows(t):
            th1 = correction(t, 1)
            score(t, 1)
            add_correction(t, 1, th1)

        def look(t, cols):
            entries = slice(cols.start // 16, cols.stop // 16)
            seen = ring.tile([P, cols.stop - cols.start], F32, name="seen")
            nc.scalar.activation(
                out=seen[:], in_=e[t][:].indirect(pos1_sb[:, entries]), func=ACT.Sigmoid, bias=thr_sb[:, t : t + 1]
            )
            weighted = ring.tile([P, cols.stop - cols.start], F32, name="weighted")
            if t < VECTOR_WEIGHS:
                nc.vector.tensor_scalar(
                    out=weighted[:], in0=seen[:], scalar1=sgg[:, t : t + 1], scalar2=None, op0=ALU.mult
                )
            else:
                nc.scalar.activation(out=weighted[:], in_=seen[:], func=ACT.Copy, scale=sgg[:, t : t + 1])
            return weighted

        def pick(t, cols):
            picked = ring.tile([P, cols.stop - cols.start], F32, name="picked")
            nc.vector.tensor_copy(picked[:], d[t][:].indirect(pos2_sb[:, cols.start // 16 : cols.stop // 16]))
            return picked

        def combine(t, cols, picked, weighted):
            nc.vector.scalar_tensor_tensor(
                out=y[:, t, cols],
                in0=picked[:],
                scalar=gain_sb[:, t : t + 1],
                in1=weighted[:],
                op0=ALU.mult,
                op1=ALU.add,
            )
            nc.sync.dma_start(out=y_out[:, t, cols], in_=y[:, t, cols])

        whole = slice(0, M)
        halves = [slice(0, M // 2), slice(M // 2, M)]
        finish_rows(0)
        for t in range(PACK - 1):
            picked = pick(t, whole)
            finish_rows(t + 1)
            combine(t, whole, picked, look(t, whole))
        picked = [pick(PACK - 1, cols) for cols in halves]
        for i, cols in enumerate(halves):
            combine(PACK - 1, cols, picked[i], look(PACK - 1, cols))
        for i in range(2):
            cols = slice(i * M // 2, (i + 1) * M // 2)
            copy = nc.vector.tensor_copy if i else nc.scalar.copy
            copy(
                out=yb[:, cols, :].rearrange("p (c i) t -> p c t i", i=4),
                in_=y[:, :, cols].rearrange("p t (c i) -> p c t i", i=4),
            )
            nc.vector.quantize_mx(
                out=y_words[:, cols].bitcast(FP8X4),
                scales=y_plane[:, cols],
                in_=yb[:, cols, :].rearrange("p m t -> p (m t)"),
            )
            nc.sync.dma_start(out=words_out[:, cols], in_=y_words[:, cols].bitcast(I32))
        for q in range(4):
            queue = nc.scalar if q % 2 else nc.sync
            queue.dma_start(
                out=out_2[0, 4 * q : 4 * q + 4, :].bitcast(I32), in_=y_plane[32 * q : 32 * q + 4, :].bitcast(I32)
            )
